import numpy as np
import ml_dtypes


def mxq(x, axis, fmt="e4m3"):
    dtype, down = {"e4m3": (ml_dtypes.float8_e4m3fn, 7), "e5m2": (ml_dtypes.float8_e5m2, 14)}[fmt]
    v = np.moveaxis(np.asarray(x, np.float32).astype(ml_dtypes.bfloat16).astype(np.float64), axis, -1)
    blocks = v.reshape(v.shape[:-1] + (-1, 32))
    amax = np.abs(blocks).max(-1, keepdims=True)
    byte = np.maximum(np.where(amax > 0, np.frexp(amax)[1] - 1 + 127, 0) - down, 1)
    scale = np.exp2(byte - 127.0)
    codes = (blocks / scale).astype(np.float32).astype(dtype).astype(np.float64)
    return np.moveaxis((codes * scale).reshape(v.shape), -1, axis)


WIDE = False


def mx_kscale(k):
    if not WIDE:
        return np.ones(k)
    levels = np.array([30, -30])
    if k % 512:
        return np.exp2(np.random.permutation(np.resize(levels, k // 32))).repeat(32)
    a = np.empty((k // 512, 16))
    for p in range(k // 512):
        a[p, :8] = np.random.permutation(np.resize(levels, 8))
        for g in range(8):
            far = levels[np.abs(levels - a[p, g]) >= 10]
            a[p, g + 8] = far[np.random.randint(len(far))]
    return np.exp2(a.ravel()).repeat(32)


def f64(x):
    return np.asarray(x).astype(np.float64)


def striped(idx):
    return np.tile(np.asarray(idx).reshape(-1, 16).T, (8, 1)).astype(np.uint16)


def unstriped(offs):
    return offs[:16].T.reshape(-1).astype(np.int64)


def striped8(idx):
    return np.asarray(idx).reshape(8, -1, 16).transpose(0, 2, 1).reshape(128, -1).astype(np.uint16)


def unstriped8(offs):
    return offs.reshape(8, 16, -1).transpose(0, 2, 1).reshape(8, -1).astype(np.int64)


def pick8(x, idx, run):
    r = np.arange(len(x))
    return x[r[:, None], idx[r % (8 * run) // run]]


E2M1 = np.array([0.0, 0.5, 1.0, 1.5, 2.0, 3.0, 4.0, 6.0, -0.0, -0.5, -1.0, -1.5, -2.0, -3.0, -4.0, -6.0])


def pack_weight(w, fmt):
    k, n = w.shape
    w = f64(np.asarray(w, np.float32).astype(ml_dtypes.bfloat16)).reshape(k // 32, 32, n)
    amax = np.abs(w).max(1)
    if fmt in ("e4m3", "e5m2"):
        byte = np.frexp(amax)[1] - 1 + 127 - (7 if fmt == "e4m3" else 14)
    else:
        mant, ex = np.frexp(amax / 6.0)
        byte = np.where(mant > 0.5, ex, ex - 1) + 127
    byte = np.clip(np.where(amax > 0, byte, 1), 1, 254)
    scaled = (w * np.exp2(127.0 - byte)[:, None, :]).reshape(k, n).astype(np.float32)
    by_word = np.ascontiguousarray(scaled.reshape(k // 512, 128, 4, n).transpose(0, 1, 3, 2))
    if fmt in ("e4m3", "e5m2"):
        words = by_word.astype(ml_dtypes.float8_e4m3fn if fmt == "e4m3" else ml_dtypes.float8_e5m2).view(np.uint8)
    else:
        c = by_word.astype(ml_dtypes.float4_e2m1fn).view(np.uint8) & 0xF
        words = (c[..., 0::2] | (c[..., 1::2] << 4)).reshape(k // 512, 128, 2 * n)
    return np.ascontiguousarray(words), np.ascontiguousarray(byte.astype(np.uint8).reshape(k // 512, 16, n))


def unpack_weight(words, scales, fmt):
    g, _, n = scales.shape
    words = np.ascontiguousarray(words).reshape(g, 128, n, -1)
    if fmt in ("e4m3", "e5m2"):
        vals = words.view(ml_dtypes.float8_e4m3fn if fmt == "e4m3" else ml_dtypes.float8_e5m2).astype(np.float64)
    else:
        nib = np.empty((g, 128, n, 4), np.uint8)
        nib[..., 0::2] = words & 0xF
        nib[..., 1::2] = words >> 4
        vals = E2M1[nib]
    vals = vals * np.repeat(np.exp2(scales.astype(np.float64) - 127.0), 8, axis=1)[..., None]
    return vals.transpose(0, 1, 3, 2).reshape(g * 512, n)


K, T, J, R, F, Z, C, O, N, S, E = 512, 1024, 256, 512, 512, 1024, 512, 128, 256, 1024, 1024


def setup_inputs():
    n = np.random.standard_normal
    idx = np.random.permutation(T)[:J]
    idx2 = np.random.permutation(Z)[:J]
    idx3 = np.stack([np.random.permutation(C)[:J] for _ in range(8)])
    idx4 = np.stack([np.random.permutation(C)[:O] for _ in range(8)])
    idx5 = np.random.permutation(J)[:O]
    idx6 = np.random.permutation(S)[:N]
    idx7 = np.random.permutation(E)[:O]
    fk = mx_kscale(K)
    ff = mx_kscale(F)
    fr = mx_kscale(R)
    xtp = pack_weight(n((K, T)) / fk[:, None], "e4m3")
    xop = pack_weight(n((F, Z)) / ff[:, None], "e2m1")
    wp = pack_weight(n((K, R)) * 1 / np.sqrt(K) * fk[:, None] * fr, "e2m1")
    w0p = pack_weight(n((F, R)) * 1 / np.sqrt(F) * ff[:, None] * fr, "e5m2")
    w2p = pack_weight(n((F, R)) * 1 / np.sqrt(F) * ff[:, None], "e5m2")
    vsp = pack_weight(n((R, S)) * 1 / np.sqrt(R) / fr[:, None], "e5m2")
    return {
        "xt_words": xtp[0],
        "xt_scales": xtp[1],
        "xo_words": xop[0],
        "xo_scales": xop[1],
        "w_words": wp[0],
        "w_scales": wp[1],
        "w0_words": w0p[0],
        "w0_scales": w0p[1],
        "w2_words": w2p[0],
        "w2_scales": w2p[1],
        "vs_words": vsp[0],
        "vs_scales": vsp[1],
        "offs": striped(idx),
        "offs2": striped(idx2),
        "offs3": striped8(idx3),
        "offs4": striped8(idx4),
        "offs5": striped(idx5),
        "offs6": striped(idx6),
        "offs7": striped(idx7),
    }


def reference(xt_words, xt_scales, xo_words, xo_scales, w_words, w_scales, w0_words, w0_scales, w2_words, w2_scales, vs_words, vs_scales, offs, offs2, offs3, offs4, offs5, offs6, offs7):
    idx = unstriped(offs)
    idx2 = unstriped(offs2)
    idx3 = unstriped8(offs3)
    idx4 = unstriped8(offs4)
    idx5 = unstriped(offs5)
    idx6 = unstriped(offs6)
    idx7 = unstriped(offs7)
    xtu = unpack_weight(xt_words, xt_scales, "e4m3")
    xou = unpack_weight(xo_words, xo_scales, "e2m1")
    wu = unpack_weight(w_words, w_scales, "e2m1")
    w0u = unpack_weight(w0_words, w0_scales, "e5m2")
    w2u = unpack_weight(w2_words, w2_scales, "e5m2")
    vsu = unpack_weight(vs_words, vs_scales, "e5m2")
    xtidxg = xtu[:, idx]
    xoidx2g = xou[:, idx2]
    a = wu.T @ xtidxg + w0u.T @ xoidx2g
    b = w2u.T @ xoidx2g
    lb = b[:, 0:1]
    la = a[:, 0:1]
    pw = np.zeros((R, C))
    pw[np.arange(R)[:, None], idx3[np.arange(R) % 512 // 64]] = a
    hid = np.abs(pick8(pw, idx4, 64) * lb - b[:, idx5] * la)
    vsidx6g = vsu[:, idx6]
    hidq = mxq(hid, 0, "e4m3")
    p = vsidx6g.T @ hidq
    y = np.zeros((N, E))
    y[:, idx7] = p
    return y

@@ -1,0 +1,190 @@
+from contextlib import ExitStack
+
+import concourse.mybir as mybir
+
+K, T, J, R, Z, C, O, N, S, E = 512, 1024, 256, 512, 1024, 512, 128, 256, 1024, 1024
+FLOPS = 3 * 2 * K * R * J + 2 * R * N * O
+
+F32 = mybir.dt.float32
+BF16 = mybir.dt.bfloat16
+I32 = mybir.dt.int32
+U32 = mybir.dt.uint32
+U16 = mybir.dt.uint16
+U8 = mybir.dt.uint8
+E4M3 = mybir.dt.float8_e4m3fn_x4
+E5M2 = mybir.dt.float8_e5m2_x4
+E2M1 = mybir.dt.float4_e2m1fn_x4
+ACT = mybir.ActivationFunctionType
+ALU = mybir.AluOpType
+
+P = 128
+PACK = 4
+QUADS = 4
+
+
+def tile_list_leadgroupboard_noted_store_scattered_kernel(
+    tc, xt_words, xt_scales, xo_words, xo_scales, w_words, w_scales, w0_words, w0_scales,
+    w2_words, w2_scales, vs_words, vs_scales, offs, offs2, offs3, offs4, offs5, offs6, offs7, out,
+):
+    nc = tc.nc
+    with ExitStack() as ctx:
+        lists = ctx.enter_context(tc.tile_pool(name="lists", bufs=1))
+        sb = ctx.enter_context(tc.tile_pool(name="sb", bufs=1))
+        held = ctx.enter_context(tc.tile_pool(name="held", bufs=1))
+        ps = ctx.enter_context(tc.psum_pool(name="ps", bufs=1))
+
+        def load_list(src, name):
+            t = lists.tile(list(src.shape), U16, name=name)
+            nc.sync.dma_start(t[:], src)
+            return t
+
+        def load_words8(src, cols, name):
+            t = sb.tile([P, cols], I32, name=name, align_bytes=64)
+            nc.sync.dma_start(t[:], src[0].rearrange("p n t -> p (n t)").bitcast(I32))
+            return t
+
+        def load_words4(src, cols, name):
+            t = sb.tile([P, cols], U16, name=name, align_bytes=64)
+            nc.sync.dma_start(t[:].bitcast(I32), src[0].bitcast(I32))
+            return t
+
+        def zeroed_bytes(cols, name):
+            t = sb.tile([P, cols], U8, name=name, align_bytes=64)
+            nc.vector.memset(t[:].bitcast(I32), 0)
+            return t
+
+        def load_scale_rows(dst, src):
+            for q in range(QUADS):
+                nc.sync.dma_start(dst[32 * q : 32 * q + 4, :].bitcast(I32), src[0, 4 * q : 4 * q + 4, :].bitcast(I32))
+
+        ws = sb.tile([P, 2, 3, R], U8, name="ws", align_bytes=64)
+        nc.vector.memset(ws[0:64].rearrange("p s w n -> p (s w n)").bitcast(I32), 0)
+        xo_s = zeroed_bytes(Z, "xo_s")
+        xt_s = held.tile([P, T], U8, name="xt_s", offset=4 * E - T // 2)
+        nc.vector.memset(xt_s[:].bitcast(I32), 0)
+        vs_s = zeroed_bytes(S, "vs_s")
+
+        xo_w = load_words4(xo_words, Z, "xo_w")
+        for i, src in enumerate((w_scales, w0_scales, w2_scales)):
+            rows = src[0].rearrange("(s u r) n -> u r s n", s=2, u=2)
+            for u in range(2):
+                nc.sync.dma_start(ws[32 * u : 32 * u + 4, :, i, :].bitcast(I32), rows[u].bitcast(I32))
+        l2 = load_list(offs2, "l2")
+        load_scale_rows(xo_s, xo_scales)
+        w0_w = load_words8(w0_words, R, "w0_w")
+        xt_w = load_words8(xt_words, T, "xt_w")
+        l1 = load_list(offs, "l1")
+        w_w = load_words4(w_words, R, "w_w")
+        load_scale_rows(xt_s, xt_scales)
+        w2_w = load_words8(w2_words, R, "w2_w")
+        l3 = load_list(offs3, "l3")
+        l5 = load_list(offs5, "l5")
+        l4 = load_list(offs4, "l4")
+        vs_w = load_words8(vs_words, S, "vs_w")
+        l6 = load_list(offs6, "l6")
+        load_scale_rows(vs_s, vs_scales)
+        l7 = load_list(offs7, "l7")
+
+        boards = []
+        for t in range(PACK):
+            bd = sb.tile([P, C], F32, name=f"board{t}")
+            nc.vector.memset(bd[:], 0.0)
+            boards.append(bd)
+
+        nc.vector.tensor_copy(
+            ws[64:128, 0].rearrange("p w n -> p (w n)").bitcast(I32),
+            ws[0:64, 1].rearrange("p w n -> p (w n)").bitcast(I32),
+        )
+        ws_d = sb.tile([P, 3, PACK, P], U8, name="ws_d", align_bytes=64)
+        nc.vector.tensor_copy(
+            ws_d[:].rearrange("p w t (b i) -> p w b t i", i=16),
+            ws[:, 0].rearrange("p w (b i t) -> p w b t i", i=16, t=PACK),
+        )
+
+        def gather(window, offsets, n, dtype, name, tag=None):
+            g = sb.tile([P, n], dtype, name=name, tag=tag or name, align_bytes=64)
+            nc.vector.tensor_copy(g[:], window.indirect(offsets[:]))
+            return g
+
+        xo_gw = gather(xo_w[:], l2, J, U16, "xo_gw")
+        xo_gs = gather(xo_s[:], l2, J, U8, "xo_gs")
+        xt_gw = gather(xt_w[:].bitcast(U32), l1, J, U32, "xt_gw")
+        xt_gs = gather(xt_s[:], l1, J, U8, "xt_gs")
+
+        def deal_words(src, dtype, run, name):
+            d = sb.tile([P, PACK, P], dtype, name=name, align_bytes=64)
+            nc.scalar.copy(
+                d[:].rearrange("p t (b i) -> p b t i", i=run),
+                src.rearrange("p (b i t) -> p b t i", i=run, t=PACK),
+            )
+            return d
+
+        w0_d = deal_words(w0_w[:].bitcast(U32), U32, 4, "w0_d")
+        w_d = deal_words(w_w[:], U16, 8, "w_d")
+        w2_d = deal_words(w2_w[:].bitcast(U32), U32, 4, "w2_d")
+
+        pages = []
+        for h in range(N // P):
+            pg = held.tile([P, E], F32, name=f"page{h}", offset=4 * E * h)
+            nc.vector.memset(pg[:], 0.0)
+            pages.append(pg)
+
+        a_ps = [ps.tile([P, J], F32, name=f"a_ps{t}") for t in range(PACK)]
+        b_ps = [ps.tile([P, 2, J], F32, name=f"b_ps{u}") for u in range(2)]
+        for t in range(PACK):
+            nc.tensor.matmul_mx(out=a_ps[t][:], lhsT=w0_d[:, t, :].bitcast(E5M2), lhsT_scale=ws_d[:, 1, t, :],
+                                rhs=xo_gw[:].bitcast(E2M1), rhs_scale=xo_gs[:], start=True, stop=False)
+        a_sb = []
+        for t in range(PACK):
+            nc.tensor.matmul_mx(out=a_ps[t][:], lhsT=w_d[:, t, :].bitcast(E2M1), lhsT_scale=ws_d[:, 0, t, :],
+                                rhs=xt_gw[:].bitcast(E4M3), rhs_scale=xt_gs[:], start=False, stop=True)
+            a_t = sb.tile([P, J], F32, name=f"a{t}", tag=f"a{t}", align_bytes=64)
+            nc.scalar.activation(a_t[:], a_ps[t][:], ACT.Copy)
+            nc.vector.tensor_copy(boards[t][:].indirect(l3[:]), a_t[:])
+            a_sb.append(a_t)
+
+        b_sb = []
+        for t in range(PACK):
+            nc.tensor.matmul_mx(out=b_ps[t // 2][:, t % 2, :], lhsT=w2_d[:, t, :].bitcast(E5M2), lhsT_scale=ws_d[:, 2, t, :],
+                                rhs=xo_gw[:].bitcast(E2M1), rhs_scale=xo_gs[:], start=True, stop=True)
+        for t in range(PACK):
+            b_t = sb.tile([P, J], F32, name=f"b{t}")
+            nc.scalar.activation(b_t[:], b_ps[t // 2][:, t % 2, :], ACT.Copy)
+            b_sb.append(b_t)
+
+        hid = sb.tile([P, O, PACK], BF16, name="hid", align_bytes=64)
+        ys = []
+        for t in range(PACK):
+            y_t = sb.tile([P, O], F32, name=f"y{t}", tag=f"y{t}", align_bytes=64)
+            nc.scalar.activation(y_t[:], b_sb[t][:].indirect(l5[:]), ACT.Copy, scale=a_sb[t][:, 0:1])
+            ys.append(y_t)
+        for u in range(2):
+            d_u = sb.tile([P, 2, O], F32, name=f"d{u}")
+            for v in range(2):
+                t = 2 * u + v
+                x_t = sb.tile([P, O], F32, name=f"x{t}")
+                nc.scalar.activation(x_t[:], boards[t][:].indirect(l4[:]), ACT.Copy, scale=b_sb[t][:, 0:1])
+                if t == PACK - 1:
+                    vs_gw = gather(vs_w[:].bitcast(U32), l6, N, U32, "vs_gw", tag=f"a{t}")
+                nc.vector.tensor_tensor(d_u[:, v, :], x_t[:], ys[t][:], ALU.subtract)
+            nc.scalar.activation(hid[:, :, 2 * u : 2 * u + 2], d_u[:].rearrange("p t o -> p o t"), ACT.Abs)
+        vs_gs = gather(vs_s[:], l6, N, U8, "vs_gs", tag=f"y{PACK - 1}")
+
+        hq_w = sb.tile([P, O], U32, name="hq_w", align_bytes=64)
+        hq_s = sb.tile([P, O], U8, name="hq_s", align_bytes=64)
+        nc.vector.quantize_mx(out=hq_w[:].bitcast(E4M3), scales=hq_s[:], in_=hid[:].rearrange("p o t -> p (o t)"))
+
+        for h in range(N // P):
+            acc = ps.tile([P, O], F32, name=f"p_ps{h}")
+            cols = slice(h * P, (h + 1) * P)
+            nc.tensor.matmul_mx(out=acc[:], lhsT=vs_gw[:, cols].bitcast(E5M2), lhsT_scale=vs_gs[:, cols],
+                                rhs=hq_w[:].bitcast(E4M3), rhs_scale=hq_s[:], start=True, stop=True)
+            p_h = sb.tile([P, O], F32, name=f"p{h}")
+            if h == 0:
+                nc.scalar.activation(p_h[:], acc[:], ACT.Copy)
+                nc.scalar.activation(pages[h][:].indirect(l7[:]), p_h[:], ACT.Copy)
+                nc.scalar.dma_start(out[cols, :], pages[h][:])
+            else:
+                nc.vector.tensor_copy(p_h[:], acc[:])
+                nc.vector.tensor_copy(pages[h][:].indirect(l7[:]), p_h[:])
+                nc.sync.dma_start(out[cols, :], pages[h][:])

@@ -30,7 +30,6 @@ def tile_list_leadgroupboard_noted_store_scattered_kernel(
     with ExitStack() as ctx:
         lists = ctx.enter_context(tc.tile_pool(name="lists", bufs=1))
         sb = ctx.enter_context(tc.tile_pool(name="sb", bufs=1))
-        held = ctx.enter_context(tc.tile_pool(name="held", bufs=1))
         ps = ctx.enter_context(tc.psum_pool(name="ps", bufs=1))
 
         def load_list(src, name):
@@ -48,21 +47,20 @@ def tile_list_leadgroupboard_noted_store_scattered_kernel(
             nc.sync.dma_start(t[:].bitcast(I32), src[0].bitcast(I32))
             return t
 
-        def zeroed_bytes(cols, name):
-            t = sb.tile([P, cols], U8, name=name, align_bytes=64)
+        def zeroed_bytes(cols, name, tag):
+            t = sb.tile([P, cols], U8, name=name, tag=tag, align_bytes=64)
             nc.vector.memset(t[:].bitcast(I32), 0)
             return t
 
-        def load_scale_rows(dst, src):
+        def load_scale_rows(queue, dst, src):
             for q in range(QUADS):
-                nc.sync.dma_start(dst[32 * q : 32 * q + 4, :].bitcast(I32), src[0, 4 * q : 4 * q + 4, :].bitcast(I32))
+                queue.dma_start(dst[32 * q : 32 * q + 4, :].bitcast(I32), src[0, 4 * q : 4 * q + 4, :].bitcast(I32))
 
         ws = sb.tile([P, 2, 3, R], U8, name="ws", align_bytes=64)
         nc.vector.memset(ws[0:64].rearrange("p s w n -> p (s w n)").bitcast(I32), 0)
-        xo_s = zeroed_bytes(Z, "xo_s")
-        xt_s = held.tile([P, T], U8, name="xt_s", offset=4 * E - T // 2)
-        nc.vector.memset(xt_s[:].bitcast(I32), 0)
-        vs_s = zeroed_bytes(S, "vs_s")
+        xo_s = zeroed_bytes(Z, "xo_s", "after_xo_s")
+        xt_s = zeroed_bytes(T, "xt_s", "after_xt_s")
+        vs_s = zeroed_bytes(S, "vs_s", "vs_s")
 
         xo_w = load_words4(xo_words, Z, "xo_w")
         for i, src in enumerate((w_scales, w0_scales, w2_scales)):
@@ -70,19 +68,19 @@ def tile_list_leadgroupboard_noted_store_scattered_kernel(
             for u in range(2):
                 nc.sync.dma_start(ws[32 * u : 32 * u + 4, :, i, :].bitcast(I32), rows[u].bitcast(I32))
         l2 = load_list(offs2, "l2")
-        load_scale_rows(xo_s, xo_scales)
         w0_w = load_words8(w0_words, R, "w0_w")
-        xt_w = load_words8(xt_words, T, "xt_w")
+        load_scale_rows(nc.sync, xo_s, xo_scales)
         l1 = load_list(offs, "l1")
+        xt_w = load_words8(xt_words, T, "xt_w")
         w_w = load_words4(w_words, R, "w_w")
-        load_scale_rows(xt_s, xt_scales)
-        w2_w = load_words8(w2_words, R, "w2_w")
+        load_scale_rows(nc.sync, xt_s, xt_scales)
+        l6 = load_list(offs6, "l6")
+        vs_w = load_words8(vs_words, S, "vs_w")
         l3 = load_list(offs3, "l3")
+        w2_w = load_words8(w2_words, R, "w2_w")
         l5 = load_list(offs5, "l5")
         l4 = load_list(offs4, "l4")
-        vs_w = load_words8(vs_words, S, "vs_w")
-        l6 = load_list(offs6, "l6")
-        load_scale_rows(vs_s, vs_scales)
+        load_scale_rows(nc.sync, vs_s, vs_scales)
         l7 = load_list(offs7, "l7")
 
         boards = []
@@ -90,6 +88,8 @@ def tile_list_leadgroupboard_noted_store_scattered_kernel(
             bd = sb.tile([P, C], F32, name=f"board{t}")
             nc.vector.memset(bd[:], 0.0)
             boards.append(bd)
+        page0 = sb.tile([P, E], F32, name="page0")
+        nc.vector.memset(page0[:], 0.0)
 
         nc.vector.tensor_copy(
             ws[64:128, 0].rearrange("p w n -> p (w n)").bitcast(I32),
@@ -109,10 +109,11 @@ def tile_list_leadgroupboard_noted_store_scattered_kernel(
         xo_gw = gather(xo_w[:], l2, J, U16, "xo_gw")
         xo_gs = gather(xo_s[:], l2, J, U8, "xo_gs")
         xt_gw = gather(xt_w[:].bitcast(U32), l1, J, U32, "xt_gw")
-        xt_gs = gather(xt_s[:], l1, J, U8, "xt_gs")
+        xt_gs = gather(xt_s[:], l1, J, U8, "xt_gs", tag="after_xo_s")
+        vs_gw = gather(vs_w[:].bitcast(U32), l6, N, U32, "vs_gw", tag="after_xt_s")
 
-        def deal_words(src, dtype, run, name):
-            d = sb.tile([P, PACK, P], dtype, name=name, align_bytes=64)
+        def deal_words(src, dtype, run, name, tag=None):
+            d = sb.tile([P, PACK, P], dtype, name=name, tag=tag or name, align_bytes=64)
             nc.scalar.copy(
                 d[:].rearrange("p t (b i) -> p b t i", i=run),
                 src.rearrange("p (b i t) -> p b t i", i=run, t=PACK),
@@ -120,62 +121,69 @@ def tile_list_leadgroupboard_noted_store_scattered_kernel(
             return d
 
         w0_d = deal_words(w0_w[:].bitcast(U32), U32, 4, "w0_d")
-        w_d = deal_words(w_w[:], U16, 8, "w_d")
-        w2_d = deal_words(w2_w[:].bitcast(U32), U32, 4, "w2_d")
+        w_d0 = sb.tile([P, P], U16, name="w_d0", tag="late_w2", align_bytes=64)
+        nc.scalar.copy(w_d0[:], w_w[:].rearrange("p (m t) -> p t m", t=PACK)[:, 0, :])
+        w_d = sb.tile([P, PACK - 1, P], U16, name="w_d", align_bytes=64)
+        nc.scalar.copy(
+            w_d[:].rearrange("p t (b i) -> p b t i", i=8),
+            w_w[:].rearrange("p (b i t) -> p b t i", i=8, t=PACK)[:, :, 1:PACK, :],
+        )
 
-        pages = []
-        for h in range(N // P):
-            pg = held.tile([P, E], F32, name=f"page{h}", offset=4 * E * h)
-            nc.vector.memset(pg[:], 0.0)
-            pages.append(pg)
-
-        a_ps = [ps.tile([P, J], F32, name=f"a_ps{t}") for t in range(PACK)]
-        b_ps = [ps.tile([P, 2, J], F32, name=f"b_ps{u}") for u in range(2)]
+        a_ps = [ps.tile([P, J], F32, name=f"a_ps{t}", tag=f"bank{t}") for t in range(PACK)]
         for t in range(PACK):
             nc.tensor.matmul_mx(out=a_ps[t][:], lhsT=w0_d[:, t, :].bitcast(E5M2), lhsT_scale=ws_d[:, 1, t, :],
                                 rhs=xo_gw[:].bitcast(E2M1), rhs_scale=xo_gs[:], start=True, stop=False)
-        a_sb = []
-        for t in range(PACK):
-            nc.tensor.matmul_mx(out=a_ps[t][:], lhsT=w_d[:, t, :].bitcast(E2M1), lhsT_scale=ws_d[:, 0, t, :],
+        a_sb, b_sb = [], []
+
+        def first_result(t):
+            words = w_d0[:] if t == 0 else w_d[:, t - 1, :]
+            nc.tensor.matmul_mx(out=a_ps[t][:], lhsT=words.bitcast(E2M1), lhsT_scale=ws_d[:, 0, t, :],
                                 rhs=xt_gw[:].bitcast(E4M3), rhs_scale=xt_gs[:], start=False, stop=True)
             a_t = sb.tile([P, J], F32, name=f"a{t}", tag=f"a{t}", align_bytes=64)
             nc.scalar.activation(a_t[:], a_ps[t][:], ACT.Copy)
             nc.vector.tensor_copy(boards[t][:].indirect(l3[:]), a_t[:])
             a_sb.append(a_t)
 
-        b_sb = []
-        for t in range(PACK):
-            nc.tensor.matmul_mx(out=b_ps[t // 2][:, t % 2, :], lhsT=w2_d[:, t, :].bitcast(E5M2), lhsT_scale=ws_d[:, 2, t, :],
+        def second_result(t, w2_d):
+            acc = ps.tile([P, J], F32, name=f"b_ps{t}")
+            nc.tensor.matmul_mx(out=acc[:], lhsT=w2_d[:, t, :].bitcast(E5M2), lhsT_scale=ws_d[:, 2, t, :],
                                 rhs=xo_gw[:].bitcast(E2M1), rhs_scale=xo_gs[:], start=True, stop=True)
-        for t in range(PACK):
             b_t = sb.tile([P, J], F32, name=f"b{t}")
-            nc.scalar.activation(b_t[:], b_ps[t // 2][:, t % 2, :], ACT.Copy)
+            nc.scalar.activation(b_t[:], acc[:], ACT.Copy)
             b_sb.append(b_t)
 
-        hid = sb.tile([P, O, PACK], BF16, name="hid", align_bytes=64)
-        ys = []
-        for t in range(PACK):
-            y_t = sb.tile([P, O], F32, name=f"y{t}", tag=f"y{t}", align_bytes=64)
-            nc.scalar.activation(y_t[:], b_sb[t][:].indirect(l5[:]), ACT.Copy, scale=a_sb[t][:, 0:1])
-            ys.append(y_t)
+        first_result(0)
+        w2_d = deal_words(w2_w[:].bitcast(U32), U32, 4, "w2_d", tag="late_w2")
+        for t in range(1, PACK):
+            first_result(t)
+            second_result(t - 1, w2_d)
+        second_result(PACK - 1, w2_d)
+
+        hid = sb.tile([P, O, PACK], BF16, name="hid", tag="after_hid", align_bytes=64)
         for u in range(2):
-            d_u = sb.tile([P, 2, O], F32, name=f"d{u}")
+            x_u = sb.tile([P, 2, O], F32, name=f"x{u}", tag=f"x{u}", align_bytes=64)
+            y_u = sb.tile([P, 2, O], F32, name=f"y{u}")
             for v in range(2):
                 t = 2 * u + v
-                x_t = sb.tile([P, O], F32, name=f"x{t}")
-                nc.scalar.activation(x_t[:], boards[t][:].indirect(l4[:]), ACT.Copy, scale=b_sb[t][:, 0:1])
-                if t == PACK - 1:
-                    vs_gw = gather(vs_w[:].bitcast(U32), l6, N, U32, "vs_gw", tag=f"a{t}")
-                nc.vector.tensor_tensor(d_u[:, v, :], x_t[:], ys[t][:], ALU.subtract)
+                nc.scalar.activation(y_u[:, v, :], b_sb[t][:].indirect(l5[:]), ACT.Copy, scale=a_sb[t][:, 0:1])
+            for v in range(2):
+                t = 2 * u + v
+                nc.scalar.activation(x_u[:, v, :], boards[t][:].indirect(l4[:]), ACT.Copy, scale=b_sb[t][:, 0:1])
+            d_u = sb.tile([P, 2, O], F32, name=f"d{u}")
+            nc.vector.tensor_tensor(d_u[:], x_u[:], y_u[:], ALU.subtract)
             nc.scalar.activation(hid[:, :, 2 * u : 2 * u + 2], d_u[:].rearrange("p t o -> p o t"), ACT.Abs)
-        vs_gs = gather(vs_s[:], l6, N, U8, "vs_gs", tag=f"y{PACK - 1}")
+        vs_gs = gather(vs_s[:], l6, N, U8, "vs_gs", tag="x1")
 
         hq_w = sb.tile([P, O], U32, name="hq_w", align_bytes=64)
         hq_s = sb.tile([P, O], U8, name="hq_s", align_bytes=64)
         nc.vector.quantize_mx(out=hq_w[:].bitcast(E4M3), scales=hq_s[:], in_=hid[:].rearrange("p o t -> p (o t)"))
 
+        page1 = sb.tile([P, E], F32, name="page1", tag="after_hid", align_bytes=64)
+        nc.vector.memset(page1[:], 0.0)
+        pages = [page0, page1]
+
         for h in range(N // P):
-            acc = ps.tile([P, O], F32, name=f"p_ps{h}")
+            acc = ps.tile([P, O], F32, name=f"p_ps{h}", tag=f"bank{h}")
             cols = slice(h * P, (h + 1) * P)
             nc.tensor.matmul_mx(out=acc[:], lhsT=vs_gw[:, cols].bitcast(E5M2), lhsT_scale=vs_gs[:, cols],
                                 rhs=hq_w[:].bitcast(E4M3), rhs_scale=hq_s[:], start=True, stop=True)

from contextlib import ExitStack

import concourse.mybir as mybir

K, T, J, R, Z, C, O, N, S, E = 512, 1024, 256, 512, 1024, 512, 128, 256, 1024, 1024
FLOPS = 3 * 2 * K * R * J + 2 * R * N * O

F32 = mybir.dt.float32
BF16 = mybir.dt.bfloat16
I32 = mybir.dt.int32
U32 = mybir.dt.uint32
U16 = mybir.dt.uint16
U8 = mybir.dt.uint8
E4M3 = mybir.dt.float8_e4m3fn_x4
E5M2 = mybir.dt.float8_e5m2_x4
E2M1 = mybir.dt.float4_e2m1fn_x4
ACT = mybir.ActivationFunctionType
ALU = mybir.AluOpType

P = 128
PACK = 4
QUADS = 4


def tile_list_leadgroupboard_noted_store_scattered_kernel(
    tc, xt_words, xt_scales, xo_words, xo_scales, w_words, w_scales, w0_words, w0_scales,
    w2_words, w2_scales, vs_words, vs_scales, offs, offs2, offs3, offs4, offs5, offs6, offs7, out,
):
    nc = tc.nc
    with ExitStack() as ctx:
        lists = ctx.enter_context(tc.tile_pool(name="lists", bufs=1))
        sb = ctx.enter_context(tc.tile_pool(name="sb", bufs=1))
        ps = ctx.enter_context(tc.psum_pool(name="ps", bufs=1))

        def load_list(src, name):
            t = lists.tile(list(src.shape), U16, name=name)
            nc.sync.dma_start(t[:], src)
            return t

        def load_words8(src, cols, name):
            t = sb.tile([P, cols], I32, name=name, align_bytes=64)
            nc.sync.dma_start(t[:], src[0].rearrange("p n t -> p (n t)").bitcast(I32))
            return t

        def load_words4(src, cols, name):
            t = sb.tile([P, cols], U16, name=name, align_bytes=64)
            nc.sync.dma_start(t[:].bitcast(I32), src[0].bitcast(I32))
            return t

        def zeroed_bytes(cols, name, tag):
            t = sb.tile([P, cols], U8, name=name, tag=tag, align_bytes=64)
            nc.vector.memset(t[:].bitcast(I32), 0)
            return t

        def load_scale_rows(queue, dst, src):
            for q in range(QUADS):
                queue.dma_start(dst[32 * q : 32 * q + 4, :].bitcast(I32), src[0, 4 * q : 4 * q + 4, :].bitcast(I32))

        ws = sb.tile([P, 2, 3, R], U8, name="ws", align_bytes=64)
        nc.vector.memset(ws[0:64].rearrange("p s w n -> p (s w n)").bitcast(I32), 0)
        xo_s = zeroed_bytes(Z, "xo_s", "after_xo_s")
        xt_s = zeroed_bytes(T, "xt_s", "after_xt_s")
        vs_s = zeroed_bytes(S, "vs_s", "vs_s")

        xo_w = load_words4(xo_words, Z, "xo_w")
        for i, src in enumerate((w_scales, w0_scales, w2_scales)):
            rows = src[0].rearrange("(s u r) n -> u r s n", s=2, u=2)
            for u in range(2):
                nc.sync.dma_start(ws[32 * u : 32 * u + 4, :, i, :].bitcast(I32), rows[u].bitcast(I32))
        l2 = load_list(offs2, "l2")
        w0_w = load_words8(w0_words, R, "w0_w")
        load_scale_rows(nc.sync, xo_s, xo_scales)
        l1 = load_list(offs, "l1")
        xt_w = load_words8(xt_words, T, "xt_w")
        w_w = load_words4(w_words, R, "w_w")
        load_scale_rows(nc.sync, xt_s, xt_scales)
        l6 = load_list(offs6, "l6")
        vs_w = load_words8(vs_words, S, "vs_w")
        l3 = load_list(offs3, "l3")
        w2_w = load_words8(w2_words, R, "w2_w")
        l5 = load_list(offs5, "l5")
        l4 = load_list(offs4, "l4")
        load_scale_rows(nc.sync, vs_s, vs_scales)
        l7 = load_list(offs7, "l7")

        boards = []
        for t in range(PACK):
            bd = sb.tile([P, C], F32, name=f"board{t}")
            nc.vector.memset(bd[:], 0.0)
            boards.append(bd)
        page0 = sb.tile([P, E], F32, name="page0")
        nc.vector.memset(page0[:], 0.0)

        nc.vector.tensor_copy(
            ws[64:128, 0].rearrange("p w n -> p (w n)").bitcast(I32),
            ws[0:64, 1].rearrange("p w n -> p (w n)").bitcast(I32),
        )
        ws_d = sb.tile([P, 3, PACK, P], U8, name="ws_d", align_bytes=64)
        nc.vector.tensor_copy(
            ws_d[:].rearrange("p w t (b i) -> p w b t i", i=16),
            ws[:, 0].rearrange("p w (b i t) -> p w b t i", i=16, t=PACK),
        )

        def gather(window, offsets, n, dtype, name, tag=None):
            g = sb.tile([P, n], dtype, name=name, tag=tag or name, align_bytes=64)
            nc.vector.tensor_copy(g[:], window.indirect(offsets[:]))
            return g

        xo_gw = gather(xo_w[:], l2, J, U16, "xo_gw")
        xo_gs = gather(xo_s[:], l2, J, U8, "xo_gs")
        xt_gw = gather(xt_w[:].bitcast(U32), l1, J, U32, "xt_gw")
        xt_gs = gather(xt_s[:], l1, J, U8, "xt_gs", tag="after_xo_s")
        vs_gw = gather(vs_w[:].bitcast(U32), l6, N, U32, "vs_gw", tag="after_xt_s")

        def deal_words(src, dtype, run, name, tag=None):
            d = sb.tile([P, PACK, P], dtype, name=name, tag=tag or name, align_bytes=64)
            nc.scalar.copy(
                d[:].rearrange("p t (b i) -> p b t i", i=run),
                src.rearrange("p (b i t) -> p b t i", i=run, t=PACK),
            )
            return d

        w0_d = deal_words(w0_w[:].bitcast(U32), U32, 4, "w0_d")
        w_d0 = sb.tile([P, P], U16, name="w_d0", tag="late_w2", align_bytes=64)
        nc.scalar.copy(w_d0[:], w_w[:].rearrange("p (m t) -> p t m", t=PACK)[:, 0, :])
        w_d = sb.tile([P, PACK - 1, P], U16, name="w_d", align_bytes=64)
        nc.scalar.copy(
            w_d[:].rearrange("p t (b i) -> p b t i", i=8),
            w_w[:].rearrange("p (b i t) -> p b t i", i=8, t=PACK)[:, :, 1:PACK, :],
        )

        a_ps = [ps.tile([P, J], F32, name=f"a_ps{t}", tag=f"bank{t}") for t in range(PACK)]
        for t in range(PACK):
            nc.tensor.matmul_mx(out=a_ps[t][:], lhsT=w0_d[:, t, :].bitcast(E5M2), lhsT_scale=ws_d[:, 1, t, :],
                                rhs=xo_gw[:].bitcast(E2M1), rhs_scale=xo_gs[:], start=True, stop=False)
        a_sb, b_sb = [], []

        def first_result(t):
            words = w_d0[:] if t == 0 else w_d[:, t - 1, :]
            nc.tensor.matmul_mx(out=a_ps[t][:], lhsT=words.bitcast(E2M1), lhsT_scale=ws_d[:, 0, t, :],
                                rhs=xt_gw[:].bitcast(E4M3), rhs_scale=xt_gs[:], start=False, stop=True)
            a_t = sb.tile([P, J], F32, name=f"a{t}", tag=f"a{t}", align_bytes=64)
            nc.scalar.activation(a_t[:], a_ps[t][:], ACT.Copy)
            nc.vector.tensor_copy(boards[t][:].indirect(l3[:]), a_t[:])
            a_sb.append(a_t)

        def second_result(t, w2_d):
            acc = ps.tile([P, J], F32, name=f"b_ps{t}")
            nc.tensor.matmul_mx(out=acc[:], lhsT=w2_d[:, t, :].bitcast(E5M2), lhsT_scale=ws_d[:, 2, t, :],
                                rhs=xo_gw[:].bitcast(E2M1), rhs_scale=xo_gs[:], start=True, stop=True)
            b_t = sb.tile([P, J], F32, name=f"b{t}")
            nc.scalar.activation(b_t[:], acc[:], ACT.Copy)
            b_sb.append(b_t)

        first_result(0)
        w2_d = deal_words(w2_w[:].bitcast(U32), U32, 4, "w2_d", tag="late_w2")
        for t in range(1, PACK):
            first_result(t)
            second_result(t - 1, w2_d)
        second_result(PACK - 1, w2_d)

        hid = sb.tile([P, O, PACK], BF16, name="hid", tag="after_hid", align_bytes=64)
        for u in range(2):
            x_u = sb.tile([P, 2, O], F32, name=f"x{u}", tag=f"x{u}", align_bytes=64)
            y_u = sb.tile([P, 2, O], F32, name=f"y{u}")
            for v in range(2):
                t = 2 * u + v
                nc.scalar.activation(y_u[:, v, :], b_sb[t][:].indirect(l5[:]), ACT.Copy, scale=a_sb[t][:, 0:1])
            for v in range(2):
                t = 2 * u + v
                nc.scalar.activation(x_u[:, v, :], boards[t][:].indirect(l4[:]), ACT.Copy, scale=b_sb[t][:, 0:1])
            d_u = sb.tile([P, 2, O], F32, name=f"d{u}")
            nc.vector.tensor_tensor(d_u[:], x_u[:], y_u[:], ALU.subtract)
            nc.scalar.activation(hid[:, :, 2 * u : 2 * u + 2], d_u[:].rearrange("p t o -> p o t"), ACT.Abs)
        vs_gs = gather(vs_s[:], l6, N, U8, "vs_gs", tag="x1")

        hq_w = sb.tile([P, O], U32, name="hq_w", align_bytes=64)
        hq_s = sb.tile([P, O], U8, name="hq_s", align_bytes=64)
        nc.vector.quantize_mx(out=hq_w[:].bitcast(E4M3), scales=hq_s[:], in_=hid[:].rearrange("p o t -> p (o t)"))

        page1 = sb.tile([P, E], F32, name="page1", tag="after_hid", align_bytes=64)
        nc.vector.memset(page1[:], 0.0)
        pages = [page0, page1]

        for h in range(N // P):
            acc = ps.tile([P, O], F32, name=f"p_ps{h}", tag=f"bank{h}")
            cols = slice(h * P, (h + 1) * P)
            nc.tensor.matmul_mx(out=acc[:], lhsT=vs_gw[:, cols].bitcast(E5M2), lhsT_scale=vs_gs[:, cols],
                                rhs=hq_w[:].bitcast(E4M3), rhs_scale=hq_s[:], start=True, stop=True)
            p_h = sb.tile([P, O], F32, name=f"p{h}")
            if h == 0:
                nc.scalar.activation(p_h[:], acc[:], ACT.Copy)
                nc.scalar.activation(pages[h][:].indirect(l7[:]), p_h[:], ACT.Copy)
                nc.scalar.dma_start(out[cols, :], pages[h][:])
            else:
                nc.vector.tensor_copy(p_h[:], acc[:])
                nc.vector.tensor_copy(pages[h][:].indirect(l7[:]), p_h[:])
                nc.sync.dma_start(out[cols, :], pages[h][:])
